import numpy as np
import ml_dtypes


def mxq(x, axis, fmt="e4m3"):
    dtype, down = {"e4m3": (ml_dtypes.float8_e4m3fn, 7), "e5m2": (ml_dtypes.float8_e5m2, 14)}[fmt]
    v = np.moveaxis(np.asarray(x, np.float32).astype(ml_dtypes.bfloat16).astype(np.float64), axis, -1)
    blocks = v.reshape(v.shape[:-1] + (-1, 32))
    amax = np.abs(blocks).max(-1, keepdims=True)
    byte = np.maximum(np.where(amax > 0, np.frexp(amax)[1] - 1 + 127, 0) - down, 1)
    scale = np.exp2(byte - 127.0)
    codes = (blocks / scale).astype(np.float32).astype(dtype).astype(np.float64)
    return np.moveaxis((codes * scale).reshape(v.shape), -1, axis)


WIDE = False


def mx_kscale(k):
    if not WIDE:
        return np.ones(k)
    levels = np.array([10, -10, 5, -5, 0])
    if k % 512:
        return np.exp2(np.random.permutation(np.resize(levels, k // 32))).repeat(32)
    a = np.empty((k // 512, 16))
    for p in range(k // 512):
        a[p, :8] = np.random.permutation(np.resize(levels, 8))
        for g in range(8):
            far = levels[np.abs(levels - a[p, g]) >= 10]
            a[p, g + 8] = far[np.random.randint(len(far))]
    return np.exp2(a.ravel()).repeat(32)


def f64(x):
    return np.asarray(x).astype(np.float64)


def striped(idx):
    return np.tile(np.asarray(idx).reshape(-1, 16).T, (8, 1)).astype(np.uint16)


def unstriped(offs):
    return offs[:16].T.reshape(-1).astype(np.int64)


E2M1 = np.array([0.0, 0.5, 1.0, 1.5, 2.0, 3.0, 4.0, 6.0, -0.0, -0.5, -1.0, -1.5, -2.0, -3.0, -4.0, -6.0])


def pack_weight(w, fmt):
    k, n = w.shape
    w = f64(np.asarray(w, np.float32).astype(ml_dtypes.bfloat16)).reshape(k // 32, 32, n)
    amax = np.abs(w).max(1)
    if fmt == "e4m3":
        byte = np.frexp(amax)[1] - 1 + 127 - 7
    else:
        mant, ex = np.frexp(amax / 6.0)
        byte = np.where(mant > 0.5, ex, ex - 1) + 127
    byte = np.clip(np.where(amax > 0, byte, 1), 1, 254)
    scaled = (w * np.exp2(127.0 - byte)[:, None, :]).reshape(k, n).astype(np.float32)
    by_word = np.ascontiguousarray(scaled.reshape(k // 512, 128, 4, n).transpose(0, 1, 3, 2))
    if fmt == "e4m3":
        words = by_word.astype(ml_dtypes.float8_e4m3fn).view(np.uint8)
    else:
        c = by_word.astype(ml_dtypes.float4_e2m1fn).view(np.uint8) & 0xF
        words = (c[..., 0::2] | (c[..., 1::2] << 4)).reshape(k // 512, 128, 2 * n)
    return np.ascontiguousarray(words), np.ascontiguousarray(byte.astype(np.uint8).reshape(k // 512, 16, n))


def unpack_weight(words, scales, fmt):
    g, _, n = scales.shape
    words = np.ascontiguousarray(words).reshape(g, 128, n, -1)
    if fmt == "e4m3":
        vals = words.view(ml_dtypes.float8_e4m3fn).astype(np.float64)
    else:
        nib = np.empty((g, 128, n, 4), np.uint8)
        nib[..., 0::2] = words & 0xF
        nib[..., 1::2] = words >> 4
        vals = E2M1[nib]
    vals = vals * np.repeat(np.exp2(scales.astype(np.float64) - 127.0), 8, axis=1)[..., None]
    return vals.transpose(0, 1, 3, 2).reshape(g * 512, n)


D, T, I, Q, E, Z, M = 512, 2048, 512, 256, 512, 1024, 1024


def setup_inputs():
    n = np.random.standard_normal
    idx = np.random.permutation(T)[:I]
    idx2 = np.random.permutation(Z)[:I]
    idx3 = np.random.permutation(Z)[:I]
    idx4 = np.random.permutation(M)[:Q]
    fd = mx_kscale(D)
    fi = mx_kscale(I)
    ti = np.ones(T)
    ti[idx] = fi
    keysp = pack_weight(n((D, T)) / fd[:, None], "e4m3")
    return {
        "query": (n((D, Q)) * 1.0 / np.sqrt(D) * fd[:, None]).astype(np.float32),
        "keys_words": keysp[0],
        "keys_scales": keysp[1],
        "os": (np.random.uniform(0.02, 0.08, (1, I)) * fi).astype(np.float32),
        "vals": (n((E, T)) / ti).astype(np.float32),
        "member": (n((E, M))).astype(np.float32),
        "mgain": np.tile(np.random.uniform(0.5, 2.0, M), (128, 1)).astype(np.float32),
        "offs": striped(idx),
        "offs2": striped(idx2),
        "offs3": striped(idx3),
        "offs4": striped(idx4),
    }


def reference(query, keys_words, keys_scales, os, vals, member, mgain, offs, offs2, offs3, offs4):
    idx = unstriped(offs)
    idx2 = unstriped(offs2)
    idx3 = unstriped(offs3)
    idx4 = unstriped(offs4)
    keysu = unpack_weight(keys_words, keys_scales, "e4m3")
    queryq = mxq(f64(query), 0, "e4m3")
    keysidxg = keysu[:, idx]
    a = queryq.T @ keysidxg
    f0 = np.zeros((Q, Z))
    f0[:, idx2] = a
    s = a + f0[:, idx3]
    w = np.maximum(s, 0.0)
    wo1 = w * f64(os)
    wt1 = wo1.T
    vt1 = f64(vals)[:, idx].T
    vt1q = mxq(vt1, 0, "e4m3")
    wt1q = mxq(wt1, 0, "e4m3")
    o = vt1q.T @ wt1q
    y = o * f64(mgain)[:1][:, idx4] + f64(member)[:, idx4]
    return y

@@ -1,0 +1,216 @@
+from contextlib import ExitStack
+
+import concourse.mybir as mybir
+from concourse.masks import make_identity
+
+D, T, I, Q, E, Z, M = 512, 2048, 512, 256, 512, 1024, 1024
+P = 128
+PACK = 4
+FLOPS = 2 * Q * I * D + 2 * E * Q * I
+
+F32 = mybir.dt.float32
+BF16 = mybir.dt.bfloat16
+I32 = mybir.dt.int32
+U32 = mybir.dt.uint32
+U16 = mybir.dt.uint16
+U8 = mybir.dt.uint8
+FP8X4 = mybir.dt.float8_e4m3fn_x4
+ALU = mybir.AluOpType
+COPY = mybir.ActivationFunctionType.Copy
+
+Q_BLOCKS = Q // P
+E_BLOCKS = E // P
+HALF = I // 2
+
+
+def tile_attend_passedthrough_bymember_lean_kernel(
+    tc, query, keys_words, keys_scales, slot_factor, vals, member, mgain, offs, offs2, offs3, offs4, out
+):
+    nc = tc.nc
+    with ExitStack() as ctx:
+        lists = ctx.enter_context(tc.tile_pool(name="lists", bufs=1))
+        sb = ctx.enter_context(tc.tile_pool(name="sb", bufs=1))
+        ps = ctx.enter_context(tc.psum_pool(name="ps", bufs=1))
+
+        token_list = lists.tile([P, I // 16], U16, name="token_list")
+        put_list = lists.tile([P, I // 16], U16, name="put_list")
+        look_list = lists.tile([P, I // 16], U16, name="look_list")
+        member_list = lists.tile([P, Q // 16], U16, name="member_list")
+
+        key_pool = sb.tile([P, T], I32, name="key_pool")
+        key_scale_pool = sb.tile([P, T], U8, name="key_scale_pool")
+        gain_pool = sb.tile([P, M], F32, name="gain_pool")
+        query_raw = sb.tile([P, PACK, Q], F32, name="query_raw")
+        factor = sb.tile([P, PACK], F32, name="factor")
+        val_pool = [sb.tile([P, T], F32, name="val_pool%d" % b, align_bytes=64) for b in range(E_BLOCKS)]
+        member_pool = [sb.tile([P, M], F32, name="member_pool%d" % b) for b in range(E_BLOCKS)]
+        places = [sb.tile([P, Z], F32, name="places%d" % h) for h in range(Q_BLOCKS)]
+        ident = sb.tile([P, P], F32, name="ident")
+
+        nc.vector.memset(key_scale_pool[:].bitcast(I32), 0)
+        nc.vector.memset(gain_pool[:], 0.0)
+        nc.sync.dma_start(query_raw[:], query.rearrange("(p j) q -> p j q", j=PACK))
+        for quad in range(4):
+            nc.sync.dma_start(
+                key_scale_pool[32 * quad : 32 * quad + 4, :].bitcast(I32),
+                keys_scales[0, 4 * quad : 4 * quad + 4, :].bitcast(I32),
+            )
+        nc.sync.dma_start(token_list[:], offs)
+        nc.sync.dma_start(key_pool[:], keys_words[0].rearrange("p n t -> p (n t)").bitcast(I32))
+        nc.sync.dma_start(put_list[:], offs2)
+        nc.sync.dma_start(member_list[:], offs4)
+        nc.sync.dma_start(gain_pool[0:1, :], mgain[0:1, :])
+        nc.sync.dma_start(look_list[:], offs3)
+        nc.sync.dma_start(factor[:], slot_factor.rearrange("o (p r) -> (o p) r", r=PACK))
+        for b in range(E_BLOCKS):
+            nc.sync.dma_start(val_pool[b][:], vals[b * P : (b + 1) * P, :])
+        for b in range(E_BLOCKS):
+            nc.sync.dma_start(member_pool[b][:], member[b * P : (b + 1) * P, :])
+        make_identity(nc, ident[:])
+        for h in range(Q_BLOCKS):
+            nc.vector.memset(places[h][:], 0.0)
+
+        key_scales = sb.tile([P, I], U8, name="key_scales", align_bytes=64)
+        nc.vector.tensor_copy(key_scales[:], key_scale_pool[:].indirect(token_list[:]))
+
+        q_codes, q_scales = [], []
+        for h in range(Q_BLOCKS):
+            q_grouped = sb.tile([P, P, PACK], BF16, name="q_grouped%d" % h, align_bytes=64)
+            src = query_raw[:, :, h * P : (h + 1) * P].rearrange("p t (c i) -> p c t i", i=4)
+            dst = q_grouped[:].rearrange("p (c i) t -> p c t i", i=4)
+            if h == 0:
+                nc.vector.tensor_copy(dst, src)
+            else:
+                nc.scalar.copy(dst, src)
+            codes = sb.tile([P, P], U32, name="q_codes%d" % h, align_bytes=64)
+            scales = sb.tile([P, P], U8, name="q_scales%d" % h, align_bytes=64)
+            nc.vector.quantize_mx(codes[:].bitcast(FP8X4), scales[:], q_grouped[:].rearrange("p q t -> p (q t)"))
+            q_codes.append(codes)
+            q_scales.append(scales)
+
+        gain_row = sb.tile([P, Q], F32, name="gain_row")
+        nc.scalar.activation(gain_row[:], gain_pool[:].indirect(member_list[:]), COPY)
+
+        scores = [sb.tile([P, I], F32, name="a%d" % h) for h in range(Q_BLOCKS)]
+        products = {}
+        for half in range(2):
+            key_codes = sb.tile([P, HALF], U32, name="key_codes%d" % half, align_bytes=64)
+            nc.vector.tensor_copy(
+                key_codes[:], key_pool[:].bitcast(U32).indirect(token_list[:, 16 * half : 16 * (half + 1)])
+            )
+            for h in range(Q_BLOCKS):
+                a_ps = ps.tile([P, HALF], F32, name="a_ps%d%d" % (h, half), tag="product", bufs=4)
+                nc.tensor.matmul_mx(
+                    a_ps[:], lhsT=q_codes[h][:].bitcast(FP8X4), lhsT_scale=q_scales[h][:],
+                    rhs=key_codes[:].bitcast(FP8X4), rhs_scale=key_scales[:, half * HALF : (half + 1) * HALF],
+                    start=True, stop=True,
+                )
+                products[h, half] = a_ps
+        for half in range(2):
+            cols = slice(half * HALF, (half + 1) * HALF)
+            entries = put_list[:, 16 * half : 16 * (half + 1)]
+            nc.vector.tensor_copy(scores[0][:, cols], products[0, half][:])
+            nc.vector.tensor_copy(places[0][:].indirect(entries), scores[0][:, cols])
+            nc.scalar.copy(scores[1][:, cols], products[1, half][:])
+            nc.scalar.activation(places[1][:].indirect(entries), scores[1][:, cols], COPY)
+        score_t = []
+        for h in range(Q_BLOCKS):
+            s_t = ps.tile([P, PACK, P], F32, name="s_t%d" % h, tag="score_t", bufs=2)
+            for r in range(PACK):
+                nc.tensor.matmul(
+                    s_t[:, r, :], scores[h][:, r:I:PACK], ident[:], start=(r == 0), stop=False, is_transpose=True
+                )
+            score_t.append(s_t)
+
+        gain_turned = ps.tile([P, Q_BLOCKS, P], F32, name="gain_turned", tag="product", bufs=4)
+        for h in range(Q_BLOCKS):
+            nc.tensor.transpose(gain_turned[:, h, :], gain_row[:, h * P : (h + 1) * P], ident[:])
+        gain_col = sb.tile([P, Q_BLOCKS], F32, name="gain_col")
+        nc.scalar.copy(gain_col[:], gain_turned[:, :, 0])
+        gain_spread = ps.tile([P, Q_BLOCKS, P], F32, name="gain_spread", tag="product", bufs=4)
+        for h in range(Q_BLOCKS):
+            nc.tensor.transpose(gain_spread[:, h, :], gain_col[:, h : h + 1].to_broadcast([P, P]), ident[:])
+        gain = sb.tile([P, Q], F32, name="gain")
+        nc.scalar.copy(gain[:], gain_spread[:].rearrange("p h q -> p (h q)"))
+
+        for h in range(Q_BLOCKS):
+            looked = sb.tile([P, I], F32, name="looked%d" % h)
+            if h == 0:
+                nc.vector.tensor_copy(looked[:], places[h][:].indirect(look_list[:]))
+            else:
+                nc.scalar.activation(looked[:], places[h][:].indirect(look_list[:]), COPY)
+            for r in range(PACK):
+                nc.tensor.matmul(
+                    score_t[h][:, r, :], looked[:, r:I:PACK], ident[:],
+                    start=False, stop=(r == PACK - 1), is_transpose=True,
+                )
+
+        def gather_values(b, turned, tag, align):
+            picked = sb.tile([P, I], BF16, name="v_picked%d" % b, tag=tag, align_bytes=align)
+            if b % 2 == 0:
+                nc.vector.tensor_copy(picked[:], val_pool[b][:].indirect(token_list[:]))
+            else:
+                nc.scalar.activation(picked[:], val_pool[b][:].indirect(token_list[:]), COPY)
+            pairs = picked[:].bitcast(F32)
+            for u in range(2):
+                nc.tensor.transpose(turned[:, b % 2, u, :], pairs[:, u : I // 2 : 2], ident[:])
+
+        v_turned = [ps.tile([P, 2, 2, P], F32, name="v_turned%d" % g, tag="turn", bufs=2) for g in range(2)]
+        gather_values(0, v_turned[0], "places0", None)
+        gather_values(1, v_turned[0], "places1", None)
+        gather_values(2, v_turned[1], "v_picked2", None)
+        gather_values(3, v_turned[1], "v_picked3", None)
+        w_grouped = [
+            sb.tile([P, P, PACK], BF16, name="w_grouped%d" % h, tag=("w_grouped0", "val_pool2")[h], align_bytes=64)
+            for h in range(Q_BLOCKS)
+        ]
+
+        w_codes = sb.tile([P, Q], U32, name="w_codes", align_bytes=64)
+        w_scales = sb.tile([P, Q], U8, name="w_scales", align_bytes=64)
+        for h in range(Q_BLOCKS):
+            nc.vector.scalar_tensor_tensor(
+                w_grouped[h][:], score_t[h][:].rearrange("p r q -> p q r"), 0.0,
+                factor[:].unsqueeze(1).to_broadcast([P, P, PACK]), ALU.max, ALU.mult,
+            )
+        for h in range(Q_BLOCKS):
+            nc.vector.quantize_mx(
+                w_codes[:, h * P : (h + 1) * P].bitcast(FP8X4), w_scales[:, h * P : (h + 1) * P],
+                w_grouped[h][:].rearrange("p q r -> p (q r)"),
+            )
+
+        v_codes, v_scales = [], []
+        for g in range(2):
+            grouped = sb.tile([P, 2, P, 2], F32, name="v_grouped%d" % g, tag=("val_pool3", "v_grouped1")[g], align_bytes=64)
+            nc.scalar.copy(grouped[:], v_turned[g][:].rearrange("p b u e -> p b e u"))
+            codes = sb.tile([P, 2 * P], U32, name="v_codes%d" % g, align_bytes=64)
+            scales = sb.tile([P, 2 * P], U8, name="v_scales%d" % g, align_bytes=64)
+            nc.vector.quantize_mx(
+                codes[:].bitcast(FP8X4), scales[:], grouped[:].rearrange("p b e u -> p (b e u)").bitcast(BF16)
+            )
+            v_codes.append(codes)
+            v_scales.append(scales)
+
+        scaled = []
+        for g in range(2):
+            o_ps = ps.tile([P, 2, Q], F32, name="o_ps%d" % g, tag="product", bufs=4)
+            for c in range(2):
+                nc.tensor.matmul_mx(
+                    o_ps[:, c, :], lhsT=v_codes[g][:, c * P : (c + 1) * P].bitcast(FP8X4),
+                    lhsT_scale=v_scales[g][:, c * P : (c + 1) * P],
+                    rhs=w_codes[:].bitcast(FP8X4), rhs_scale=w_scales[:], start=True, stop=True,
+                )
+            o_scaled = sb.tile([P, 2, Q], F32, name="o_scaled%d" % g)
+            nc.vector.tensor_tensor(o_scaled[:], o_ps[:], gain[:].unsqueeze(1).to_broadcast([P, 2, Q]), ALU.mult)
+            scaled.append(o_scaled)
+
+        for b in range(E_BLOCKS):
+            y = sb.tile([P, Q], F32, name="y%d" % b)
+            if b < E_BLOCKS - 1:
+                picked = sb.tile([P, Q], F32, name="m_picked%d" % b)
+                nc.scalar.activation(picked[:], member_pool[b][:].indirect(member_list[:]), COPY)
+                nc.vector.tensor_tensor(y[:], picked[:], scaled[b // 2][:, b % 2, :], ALU.add)
+            else:
+                nc.vector.tensor_tensor(
+                    y[:], member_pool[b][:].indirect(member_list[:]), scaled[b // 2][:, b % 2, :], ALU.add
+                )
+            nc.sync.dma_start(out[b * P : (b + 1) * P, :], y[:])

@@ -48,7 +48,7 @@ def tile_attend_passedthrough_bymember_lean_kernel(
         ident = sb.tile([P, P], F32, name="ident")
 
         nc.vector.memset(key_scale_pool[:].bitcast(I32), 0)
-        nc.vector.memset(gain_pool[:], 0.0)
+        nc.gpsimd.memset(gain_pool[:], 0.0)
         nc.sync.dma_start(query_raw[:], query.rearrange("(p j) q -> p j q", j=PACK))
         for quad in range(4):
             nc.sync.dma_start(
@@ -57,9 +57,9 @@ def tile_attend_passedthrough_bymember_lean_kernel(
             )
         nc.sync.dma_start(token_list[:], offs)
         nc.sync.dma_start(key_pool[:], keys_words[0].rearrange("p n t -> p (n t)").bitcast(I32))
-        nc.sync.dma_start(put_list[:], offs2)
         nc.sync.dma_start(member_list[:], offs4)
         nc.sync.dma_start(gain_pool[0:1, :], mgain[0:1, :])
+        nc.sync.dma_start(put_list[:], offs2)
         nc.sync.dma_start(look_list[:], offs3)
         nc.sync.dma_start(factor[:], slot_factor.rearrange("o (p r) -> (o p) r", r=PACK))
         for b in range(E_BLOCKS):
@@ -108,11 +108,11 @@ def tile_attend_passedthrough_bymember_lean_kernel(
                 products[h, half] = a_ps
         for half in range(2):
             cols = slice(half * HALF, (half + 1) * HALF)
-            entries = put_list[:, 16 * half : 16 * (half + 1)]
-            nc.vector.tensor_copy(scores[0][:, cols], products[0, half][:])
-            nc.vector.tensor_copy(places[0][:].indirect(entries), scores[0][:, cols])
-            nc.scalar.copy(scores[1][:, cols], products[1, half][:])
-            nc.scalar.activation(places[1][:].indirect(entries), scores[1][:, cols], COPY)
+            for h in range(Q_BLOCKS):
+                nc.scalar.copy(scores[h][:, cols], products[h, half][:])
+            nc.vector.tensor_copy(places[0][:].indirect(put_list[:, 16 * half : 16 * (half + 1)]), scores[0][:, cols])
+        for lo, hi in ((0, 384), (384, I)):
+            nc.scalar.activation(places[1][:].indirect(put_list[:, lo // 16 : hi // 16]), scores[1][:, lo:hi], COPY)
         score_t = []
         for h in range(Q_BLOCKS):
             s_t = ps.tile([P, PACK, P], F32, name="s_t%d" % h, tag="score_t", bufs=2)
@@ -158,14 +158,14 @@ def tile_attend_passedthrough_bymember_lean_kernel(
         v_turned = [ps.tile([P, 2, 2, P], F32, name="v_turned%d" % g, tag="turn", bufs=2) for g in range(2)]
         gather_values(0, v_turned[0], "places0", None)
         gather_values(1, v_turned[0], "places1", None)
-        gather_values(2, v_turned[1], "v_picked2", None)
+        gather_values(2, v_turned[1], "v_picked2", 64)
         gather_values(3, v_turned[1], "v_picked3", None)
         w_grouped = [
             sb.tile([P, P, PACK], BF16, name="w_grouped%d" % h, tag=("w_grouped0", "val_pool2")[h], align_bytes=64)
             for h in range(Q_BLOCKS)
         ]
 
-        w_codes = sb.tile([P, Q], U32, name="w_codes", align_bytes=64)
+        w_codes = sb.tile([P, Q], U32, name="w_codes", tag="v_picked2", align_bytes=64)
         w_scales = sb.tile([P, Q], U8, name="w_scales", align_bytes=64)
         for h in range(Q_BLOCKS):
             nc.vector.scalar_tensor_tensor(
@@ -205,12 +205,7 @@ def tile_attend_passedthrough_bymember_lean_kernel(
 
         for b in range(E_BLOCKS):
             y = sb.tile([P, Q], F32, name="y%d" % b)
-            if b < E_BLOCKS - 1:
-                picked = sb.tile([P, Q], F32, name="m_picked%d" % b)
-                nc.scalar.activation(picked[:], member_pool[b][:].indirect(member_list[:]), COPY)
-                nc.vector.tensor_tensor(y[:], picked[:], scaled[b // 2][:, b % 2, :], ALU.add)
-            else:
-                nc.vector.tensor_tensor(
-                    y[:], member_pool[b][:].indirect(member_list[:]), scaled[b // 2][:, b % 2, :], ALU.add
-                )
+            picked = sb.tile([P, Q], F32, name="m_picked%d" % b, tag="v_picked3" if b == 0 else "m_picked%d" % b)
+            nc.scalar.activation(picked[:], member_pool[b][:].indirect(member_list[:]), COPY)
+            nc.vector.tensor_tensor(y[:], picked[:], scaled[b // 2][:, b % 2, :], ALU.add)
             nc.sync.dma_start(out[b * P : (b + 1) * P, :], y[:])

@@ -49,20 +49,20 @@ def tile_attend_passedthrough_bymember_lean_kernel(
 
         nc.vector.memset(key_scale_pool[:].bitcast(I32), 0)
         nc.gpsimd.memset(gain_pool[:], 0.0)
-        nc.sync.dma_start(query_raw[:], query.rearrange("(p j) q -> p j q", j=PACK))
-        for quad in range(4):
-            nc.sync.dma_start(
-                key_scale_pool[32 * quad : 32 * quad + 4, :].bitcast(I32),
-                keys_scales[0, 4 * quad : 4 * quad + 4, :].bitcast(I32),
-            )
         nc.sync.dma_start(token_list[:], offs)
-        nc.sync.dma_start(key_pool[:], keys_words[0].rearrange("p n t -> p (n t)").bitcast(I32))
         nc.sync.dma_start(member_list[:], offs4)
+        nc.sync.dma_start(query_raw[:], query.rearrange("(p j) q -> p j q", j=PACK))
+        for row in range(4):
+            nc.sync.dma_start(
+                key_scale_pool[row:P:32, :].bitcast(I32), keys_scales[0, row:16:4, :].bitcast(I32)
+            )
+        nc.sync.dma_start(key_pool[:], keys_words[0].rearrange("p n t -> p (n t)").bitcast(I32))
         nc.sync.dma_start(gain_pool[0:1, :], mgain[0:1, :])
         nc.sync.dma_start(put_list[:], offs2)
+        nc.sync.dma_start(val_pool[0][:], vals[0:P, :])
         nc.sync.dma_start(look_list[:], offs3)
         nc.sync.dma_start(factor[:], slot_factor.rearrange("o (p r) -> (o p) r", r=PACK))
-        for b in range(E_BLOCKS):
+        for b in range(1, E_BLOCKS):
             nc.sync.dma_start(val_pool[b][:], vals[b * P : (b + 1) * P, :])
         for b in range(E_BLOCKS):
             nc.sync.dma_start(member_pool[b][:], member[b * P : (b + 1) * P, :])

from contextlib import ExitStack

import concourse.mybir as mybir
from concourse.masks import make_identity

D, T, I, Q, E, Z, M = 512, 2048, 512, 256, 512, 1024, 1024
P = 128
PACK = 4
FLOPS = 2 * Q * I * D + 2 * E * Q * I

F32 = mybir.dt.float32
BF16 = mybir.dt.bfloat16
I32 = mybir.dt.int32
U32 = mybir.dt.uint32
U16 = mybir.dt.uint16
U8 = mybir.dt.uint8
FP8X4 = mybir.dt.float8_e4m3fn_x4
ALU = mybir.AluOpType
COPY = mybir.ActivationFunctionType.Copy

Q_BLOCKS = Q // P
E_BLOCKS = E // P
HALF = I // 2


def tile_attend_passedthrough_bymember_lean_kernel(
    tc, query, keys_words, keys_scales, slot_factor, vals, member, mgain, offs, offs2, offs3, offs4, out
):
    nc = tc.nc
    with ExitStack() as ctx:
        lists = ctx.enter_context(tc.tile_pool(name="lists", bufs=1))
        sb = ctx.enter_context(tc.tile_pool(name="sb", bufs=1))
        ps = ctx.enter_context(tc.psum_pool(name="ps", bufs=1))

        token_list = lists.tile([P, I // 16], U16, name="token_list")
        put_list = lists.tile([P, I // 16], U16, name="put_list")
        look_list = lists.tile([P, I // 16], U16, name="look_list")
        member_list = lists.tile([P, Q // 16], U16, name="member_list")

        key_pool = sb.tile([P, T], I32, name="key_pool")
        key_scale_pool = sb.tile([P, T], U8, name="key_scale_pool")
        gain_pool = sb.tile([P, M], F32, name="gain_pool")
        query_raw = sb.tile([P, PACK, Q], F32, name="query_raw")
        factor = sb.tile([P, PACK], F32, name="factor")
        val_pool = [sb.tile([P, T], F32, name="val_pool%d" % b, align_bytes=64) for b in range(E_BLOCKS)]
        member_pool = [sb.tile([P, M], F32, name="member_pool%d" % b) for b in range(E_BLOCKS)]
        places = [sb.tile([P, Z], F32, name="places%d" % h) for h in range(Q_BLOCKS)]
        ident = sb.tile([P, P], F32, name="ident")

        nc.vector.memset(key_scale_pool[:].bitcast(I32), 0)
        nc.gpsimd.memset(gain_pool[:], 0.0)
        nc.sync.dma_start(token_list[:], offs)
        nc.sync.dma_start(member_list[:], offs4)
        nc.sync.dma_start(query_raw[:], query.rearrange("(p j) q -> p j q", j=PACK))
        for row in range(4):
            nc.sync.dma_start(
                key_scale_pool[row:P:32, :].bitcast(I32), keys_scales[0, row:16:4, :].bitcast(I32)
            )
        nc.sync.dma_start(key_pool[:], keys_words[0].rearrange("p n t -> p (n t)").bitcast(I32))
        nc.sync.dma_start(gain_pool[0:1, :], mgain[0:1, :])
        nc.sync.dma_start(put_list[:], offs2)
        nc.sync.dma_start(val_pool[0][:], vals[0:P, :])
        nc.sync.dma_start(look_list[:], offs3)
        nc.sync.dma_start(factor[:], slot_factor.rearrange("o (p r) -> (o p) r", r=PACK))
        for b in range(1, E_BLOCKS):
            nc.sync.dma_start(val_pool[b][:], vals[b * P : (b + 1) * P, :])
        for b in range(E_BLOCKS):
            nc.sync.dma_start(member_pool[b][:], member[b * P : (b + 1) * P, :])
        make_identity(nc, ident[:])
        for h in range(Q_BLOCKS):
            nc.vector.memset(places[h][:], 0.0)

        key_scales = sb.tile([P, I], U8, name="key_scales", align_bytes=64)
        nc.vector.tensor_copy(key_scales[:], key_scale_pool[:].indirect(token_list[:]))

        q_codes, q_scales = [], []
        for h in range(Q_BLOCKS):
            q_grouped = sb.tile([P, P, PACK], BF16, name="q_grouped%d" % h, align_bytes=64)
            src = query_raw[:, :, h * P : (h + 1) * P].rearrange("p t (c i) -> p c t i", i=4)
            dst = q_grouped[:].rearrange("p (c i) t -> p c t i", i=4)
            if h == 0:
                nc.vector.tensor_copy(dst, src)
            else:
                nc.scalar.copy(dst, src)
            codes = sb.tile([P, P], U32, name="q_codes%d" % h, align_bytes=64)
            scales = sb.tile([P, P], U8, name="q_scales%d" % h, align_bytes=64)
            nc.vector.quantize_mx(codes[:].bitcast(FP8X4), scales[:], q_grouped[:].rearrange("p q t -> p (q t)"))
            q_codes.append(codes)
            q_scales.append(scales)

        gain_row = sb.tile([P, Q], F32, name="gain_row")
        nc.scalar.activation(gain_row[:], gain_pool[:].indirect(member_list[:]), COPY)

        scores = [sb.tile([P, I], F32, name="a%d" % h) for h in range(Q_BLOCKS)]
        products = {}
        for half in range(2):
            key_codes = sb.tile([P, HALF], U32, name="key_codes%d" % half, align_bytes=64)
            nc.vector.tensor_copy(
                key_codes[:], key_pool[:].bitcast(U32).indirect(token_list[:, 16 * half : 16 * (half + 1)])
            )
            for h in range(Q_BLOCKS):
                a_ps = ps.tile([P, HALF], F32, name="a_ps%d%d" % (h, half), tag="product", bufs=4)
                nc.tensor.matmul_mx(
                    a_ps[:], lhsT=q_codes[h][:].bitcast(FP8X4), lhsT_scale=q_scales[h][:],
                    rhs=key_codes[:].bitcast(FP8X4), rhs_scale=key_scales[:, half * HALF : (half + 1) * HALF],
                    start=True, stop=True,
                )
                products[h, half] = a_ps
        for half in range(2):
            cols = slice(half * HALF, (half + 1) * HALF)
            for h in range(Q_BLOCKS):
                nc.scalar.copy(scores[h][:, cols], products[h, half][:])
            nc.vector.tensor_copy(places[0][:].indirect(put_list[:, 16 * half : 16 * (half + 1)]), scores[0][:, cols])
        for lo, hi in ((0, 384), (384, I)):
            nc.scalar.activation(places[1][:].indirect(put_list[:, lo // 16 : hi // 16]), scores[1][:, lo:hi], COPY)
        score_t = []
        for h in range(Q_BLOCKS):
            s_t = ps.tile([P, PACK, P], F32, name="s_t%d" % h, tag="score_t", bufs=2)
            for r in range(PACK):
                nc.tensor.matmul(
                    s_t[:, r, :], scores[h][:, r:I:PACK], ident[:], start=(r == 0), stop=False, is_transpose=True
                )
            score_t.append(s_t)

        gain_turned = ps.tile([P, Q_BLOCKS, P], F32, name="gain_turned", tag="product", bufs=4)
        for h in range(Q_BLOCKS):
            nc.tensor.transpose(gain_turned[:, h, :], gain_row[:, h * P : (h + 1) * P], ident[:])
        gain_col = sb.tile([P, Q_BLOCKS], F32, name="gain_col")
        nc.scalar.copy(gain_col[:], gain_turned[:, :, 0])
        gain_spread = ps.tile([P, Q_BLOCKS, P], F32, name="gain_spread", tag="product", bufs=4)
        for h in range(Q_BLOCKS):
            nc.tensor.transpose(gain_spread[:, h, :], gain_col[:, h : h + 1].to_broadcast([P, P]), ident[:])
        gain = sb.tile([P, Q], F32, name="gain")
        nc.scalar.copy(gain[:], gain_spread[:].rearrange("p h q -> p (h q)"))

        for h in range(Q_BLOCKS):
            looked = sb.tile([P, I], F32, name="looked%d" % h)
            if h == 0:
                nc.vector.tensor_copy(looked[:], places[h][:].indirect(look_list[:]))
            else:
                nc.scalar.activation(looked[:], places[h][:].indirect(look_list[:]), COPY)
            for r in range(PACK):
                nc.tensor.matmul(
                    score_t[h][:, r, :], looked[:, r:I:PACK], ident[:],
                    start=False, stop=(r == PACK - 1), is_transpose=True,
                )

        def gather_values(b, turned, tag, align):
            picked = sb.tile([P, I], BF16, name="v_picked%d" % b, tag=tag, align_bytes=align)
            if b % 2 == 0:
                nc.vector.tensor_copy(picked[:], val_pool[b][:].indirect(token_list[:]))
            else:
                nc.scalar.activation(picked[:], val_pool[b][:].indirect(token_list[:]), COPY)
            pairs = picked[:].bitcast(F32)
            for u in range(2):
                nc.tensor.transpose(turned[:, b % 2, u, :], pairs[:, u : I // 2 : 2], ident[:])

        v_turned = [ps.tile([P, 2, 2, P], F32, name="v_turned%d" % g, tag="turn", bufs=2) for g in range(2)]
        gather_values(0, v_turned[0], "places0", None)
        gather_values(1, v_turned[0], "places1", None)
        gather_values(2, v_turned[1], "v_picked2", 64)
        gather_values(3, v_turned[1], "v_picked3", None)
        w_grouped = [
            sb.tile([P, P, PACK], BF16, name="w_grouped%d" % h, tag=("w_grouped0", "val_pool2")[h], align_bytes=64)
            for h in range(Q_BLOCKS)
        ]

        w_codes = sb.tile([P, Q], U32, name="w_codes", tag="v_picked2", align_bytes=64)
        w_scales = sb.tile([P, Q], U8, name="w_scales", align_bytes=64)
        for h in range(Q_BLOCKS):
            nc.vector.scalar_tensor_tensor(
                w_grouped[h][:], score_t[h][:].rearrange("p r q -> p q r"), 0.0,
                factor[:].unsqueeze(1).to_broadcast([P, P, PACK]), ALU.max, ALU.mult,
            )
        for h in range(Q_BLOCKS):
            nc.vector.quantize_mx(
                w_codes[:, h * P : (h + 1) * P].bitcast(FP8X4), w_scales[:, h * P : (h + 1) * P],
                w_grouped[h][:].rearrange("p q r -> p (q r)"),
            )

        v_codes, v_scales = [], []
        for g in range(2):
            grouped = sb.tile([P, 2, P, 2], F32, name="v_grouped%d" % g, tag=("val_pool3", "v_grouped1")[g], align_bytes=64)
            nc.scalar.copy(grouped[:], v_turned[g][:].rearrange("p b u e -> p b e u"))
            codes = sb.tile([P, 2 * P], U32, name="v_codes%d" % g, align_bytes=64)
            scales = sb.tile([P, 2 * P], U8, name="v_scales%d" % g, align_bytes=64)
            nc.vector.quantize_mx(
                codes[:].bitcast(FP8X4), scales[:], grouped[:].rearrange("p b e u -> p (b e u)").bitcast(BF16)
            )
            v_codes.append(codes)
            v_scales.append(scales)

        scaled = []
        for g in range(2):
            o_ps = ps.tile([P, 2, Q], F32, name="o_ps%d" % g, tag="product", bufs=4)
            for c in range(2):
                nc.tensor.matmul_mx(
                    o_ps[:, c, :], lhsT=v_codes[g][:, c * P : (c + 1) * P].bitcast(FP8X4),
                    lhsT_scale=v_scales[g][:, c * P : (c + 1) * P],
                    rhs=w_codes[:].bitcast(FP8X4), rhs_scale=w_scales[:], start=True, stop=True,
                )
            o_scaled = sb.tile([P, 2, Q], F32, name="o_scaled%d" % g)
            nc.vector.tensor_tensor(o_scaled[:], o_ps[:], gain[:].unsqueeze(1).to_broadcast([P, 2, Q]), ALU.mult)
            scaled.append(o_scaled)

        for b in range(E_BLOCKS):
            y = sb.tile([P, Q], F32, name="y%d" % b)
            picked = sb.tile([P, Q], F32, name="m_picked%d" % b, tag="v_picked3" if b == 0 else "m_picked%d" % b)
            nc.scalar.activation(picked[:], member_pool[b][:].indirect(member_list[:]), COPY)
            nc.vector.tensor_tensor(y[:], picked[:], scaled[b // 2][:, b % 2, :], ALU.add)
            nc.sync.dma_start(out[b * P : (b + 1) * P, :], y[:])
